import numpy as np
import ml_dtypes


def mxq(x, axis, fmt="e4m3"):
    dtype, down = {"e4m3": (ml_dtypes.float8_e4m3fn, 7), "e5m2": (ml_dtypes.float8_e5m2, 14)}[fmt]
    v = np.moveaxis(np.asarray(x, np.float32).astype(ml_dtypes.bfloat16).astype(np.float64), axis, -1)
    blocks = v.reshape(v.shape[:-1] + (-1, 32))
    amax = np.abs(blocks).max(-1, keepdims=True)
    byte = np.maximum(np.where(amax > 0, np.frexp(amax)[1] - 1 + 127, 0) - down, 1)
    scale = np.exp2(byte - 127.0)
    codes = (blocks / scale).astype(np.float32).astype(dtype).astype(np.float64)
    return np.moveaxis((codes * scale).reshape(v.shape), -1, axis)


WIDE = False


def mx_kscale(k):
    if not WIDE:
        return np.ones(k)
    levels = np.array([10, -10, 5, -5, 0])
    if k % 512:
        return np.exp2(np.random.permutation(np.resize(levels, k // 32))).repeat(32)
    a = np.empty((k // 512, 16))
    for p in range(k // 512):
        a[p, :8] = np.random.permutation(np.resize(levels, 8))
        for g in range(8):
            far = levels[np.abs(levels - a[p, g]) >= 10]
            a[p, g + 8] = far[np.random.randint(len(far))]
    return np.exp2(a.ravel()).repeat(32)


def f64(x):
    return np.asarray(x).astype(np.float64)


def striped(idx):
    return np.tile(idx.reshape(-1, 16).T, (8, 1)).astype(np.uint16)


def unstriped(offs):
    return offs[:16].T.reshape(-1).astype(np.int64)


def pack_weight(w):
    k, n = w.shape
    w = f64(np.asarray(w, np.float32).astype(ml_dtypes.bfloat16)).reshape(k // 32, 32, n)
    amax = np.abs(w).max(1)
    byte = np.clip(np.where(amax > 0, np.frexp(amax)[1] - 1 + 127 - 7, 1), 1, 254)
    scaled = (w * np.exp2(127.0 - byte)[:, None, :]).reshape(k, n).astype(np.float32)
    words = np.ascontiguousarray(scaled.reshape(k // 512, 128, 4, n).transpose(0, 1, 3, 2)).astype(ml_dtypes.float8_e4m3fn).view(np.uint8)
    return words, np.ascontiguousarray(byte.astype(np.uint8).reshape(k // 512, 16, n))


def unpack_weight(words, scales):
    g, p, n, _ = words.shape
    vals = np.ascontiguousarray(words).view(ml_dtypes.float8_e4m3fn).astype(np.float64) * np.repeat(np.exp2(scales.astype(np.float64) - 127.0), 8, axis=1)[..., None]
    return vals.transpose(0, 1, 3, 2).reshape(g * 512, n)


def sigmoid(v):
    return 1.0 / (1.0 + np.exp(-np.maximum(v, -700.0)))


K, T, S, H, N, U = 512, 1024, 512, 512, 128, 1024
P = 2 ** 7


def setup_inputs():
    n = np.random.standard_normal
    s = mx_kscale(K)[:, None]
    u = mx_kscale(H)
    packed_xT = pack_weight(n((K, T)) * s)
    return {
        "x_words": packed_xT[0],
        "x_scales": packed_xT[1],
        "w1": (n((K, H)) / np.sqrt(K) / s).astype(np.float32),
        "gap": (np.tile(np.random.uniform(0.1, 2.0, S), (P, 1))).astype(np.float32),
        "base": (np.random.uniform(0.1, 0.5, (H, 1))).astype(np.float32),
        "rf": (-np.random.uniform(0.3, 2.0, (H, 1))).astype(np.float32),
        "rd": (-np.random.uniform(0.3, 2.0, (H, 1))).astype(np.float32),
        "use": (np.random.uniform(-0.1, 0.4, (H, U))).astype(np.float32),
        "gone": (np.random.uniform(0.0, 0.8, (H, U))).astype(np.float32),
        "w2": (n((H, N)) / np.sqrt(H) / u[:, None]).astype(np.float32),
        "unit": (np.random.uniform(0.5, 1.5, (H, 1)) * u[:, None]).astype(np.float32),
        "drive": (0.5 * n((N, S))).astype(np.float32),
        "offs": striped(np.random.permutation(T)[:S]),
        "slot": striped(np.random.permutation(U)[:S]),
    }


def reference(x_words, x_scales, w1, gap, base, rf, rd, use, gone, w2, unit, drive, offs, slot):
    fu = np.exp(f64(rf) * f64(gap)[:1])
    u0 = f64(use)[:, unstriped(slot)] * fu + f64(base)
    xq = unpack_weight(x_words, x_scales)[:, unstriped(offs)]
    ss = sigmoid(mxq(f64(w1), 0, "e4m3").T @ xq)
    u1 = u0 + f64(base) * (ss - (ss * u0))
    fd = np.exp(f64(rd) * f64(gap)[:1])
    x0 = -1.0 * (f64(gone)[:, unstriped(slot)] * fd) + 1.0
    rel = (u1 * x0) * ss
    z = f64(unit) * rel
    return np.tanh((mxq(f64(w2), 0, "e4m3").T @ mxq(z, 0, "e4m3")) + f64(drive))

@@ -1,0 +1,198 @@
+from contextlib import ExitStack
+
+import concourse.mybir as mybir
+
+K, T, S, H, N, U = 512, 1024, 512, 512, 128, 1024
+FLOPS = 2 * K * H * S + 2 * H * N * S
+
+F32 = mybir.dt.float32
+BF16 = mybir.dt.bfloat16
+I32 = mybir.dt.int32
+U32 = mybir.dt.uint32
+U16 = mybir.dt.uint16
+U8 = mybir.dt.uint8
+FP8X4 = mybir.dt.float8_e4m3fn_x4
+ALU = mybir.AluOpType
+ACT = mybir.ActivationFunctionType
+
+P = 128
+PACK = 4
+CHUNKS = ((0, 256), (256, 128), (384, 128))
+
+
+def tile_picked_ystp_tanh_p_kernel(
+    tc, x_words, x_scales, w1, gap, base, rf, rd, use, gone, w2, unit, drive, offs, slot, out
+):
+    nc = tc.nc
+    with ExitStack() as ctx:
+        pool = ctx.enter_context(tc.tile_pool(name="keep", bufs=1))
+        psum = ctx.enter_context(tc.psum_pool(name="psum", bufs=1))
+
+        offs_sb = pool.tile([P, S // 16], U16, name="offs_sb")
+        slot_sb = pool.tile([P, S // 16], U16, name="slot_sb")
+        xs_win = pool.tile([P, T], U8, name="xs_win")
+        xw_win = pool.tile([P, T], U32, name="xw_win")
+        gap_sb = pool.tile([P, S], F32, name="gap_sb")
+        w1_raw = [pool.tile([P, PACK, H // 2], F32, name="w1_raw%d" % h) for h in range(2)]
+        w2_raw = pool.tile([P, PACK, N], F32, name="w2_raw")
+        drive_sb = pool.tile([P, S], F32, name="drive_sb")
+        use_win = [pool.tile([P, U], F32, name="use_win%d" % t) for t in range(PACK)]
+        gone_win = [pool.tile([P, U], F32, name="gone_win%d" % t) for t in range(PACK)]
+        rf_sb = pool.tile([P, PACK], F32, name="rf_sb")
+        rd_sb = pool.tile([P, PACK], F32, name="rd_sb")
+        base_sb = pool.tile([P, PACK], F32, name="base_sb")
+        unit_sb = pool.tile([P, PACK], F32, name="unit_sb")
+
+        nc.gpsimd.memset(xs_win[:].bitcast(I32), 0)
+        for q in range(4):
+            nc.scalar.dma_start(
+                out=xs_win[32 * q : 32 * q + 4, :].bitcast(I32),
+                in_=x_scales[0, 4 * q : 4 * q + 4, :].bitcast(I32),
+            )
+        for queue, col, vec in (
+            (nc.scalar, rf_sb, rf), (nc.scalar, rd_sb, rd), (nc.gpsimd, base_sb, base), (nc.gpsimd, unit_sb, unit)
+        ):
+            queue.dma_start(out=col[:], in_=vec.rearrange("(p t) o -> p (t o)", t=PACK))
+
+        use_rows = use.rearrange("(p t) u -> p t u", t=PACK)
+        gone_rows = gone.rearrange("(p t) u -> p t u", t=PACK)
+        w1_rows = w1.rearrange("(p r) c -> p r c", r=PACK)
+        nc.sync.dma_start(offs_sb[:], offs)
+        nc.sync.dma_start(out=gap_sb[:], in_=gap)
+        nc.sync.dma_start(
+            out=xw_win[:].bitcast(I32), in_=x_words[0].rearrange("p n r -> p (n r)").bitcast(I32)
+        )
+        nc.sync.dma_start(slot_sb[:], slot)
+        nc.sync.dma_start(out=use_win[0][:], in_=use_rows[:, 0, :])
+        nc.sync.dma_start(out=w1_raw[0][:], in_=w1_rows[:, :, : H // 2])
+        nc.sync.dma_start(out=gone_win[0][:], in_=gone_rows[:, 0, :])
+        nc.sync.dma_start(out=w1_raw[1][:], in_=w1_rows[:, :, H // 2 :])
+        for t in range(1, PACK):
+            nc.sync.dma_start(out=use_win[t][:], in_=use_rows[:, t, :])
+            nc.sync.dma_start(out=gone_win[t][:], in_=gone_rows[:, t, :])
+        nc.sync.dma_start(out=w2_raw[:], in_=w2.rearrange("(p r) c -> p r c", r=PACK))
+        nc.sync.dma_start(out=drive_sb[:], in_=drive)
+
+        base_m1 = pool.tile([P, PACK], F32, name="base_m1")
+        unit_base = pool.tile([P, PACK], F32, name="unit_base")
+        neg_unit = pool.tile([P, PACK], F32, name="neg_unit")
+        nc.gpsimd.tensor_scalar(base_m1[:], base_sb[:], 1.0, -1.0, ALU.mult, ALU.add)
+        nc.gpsimd.tensor_tensor(unit_base[:], unit_sb[:], base_sb[:], ALU.mult)
+        nc.gpsimd.tensor_scalar(neg_unit[:], unit_sb[:], -1.0, 0.0, ALU.mult, ALU.add)
+
+        fu = pool.tile([P, PACK, S], F32, name="fu")
+        fd = pool.tile([P, PACK, S], F32, name="fd")
+        for t in range(PACK):
+            nc.scalar.activation(fu[:, t, :], gap_sb[:], ACT.Exp, scale=rf_sb[:, t : t + 1])
+            nc.scalar.activation(fd[:, t, :], gap_sb[:], ACT.Exp, scale=rd_sb[:, t : t + 1])
+
+        x_bytes = pool.tile([P, S], U8, name="x_bytes", align_bytes=64)
+        x_codes = pool.tile([P, S], U32, name="x_codes", align_bytes=64)
+        nc.vector.tensor_copy(x_codes[:], xw_win[:].indirect(offs_sb[:]))
+
+        used = pool.tile([P, PACK, S], F32, name="used")
+        spent = pool.tile([P, PACK, S], F32, name="spent")
+        nc.vector.tensor_tensor(used[:, 0, :], use_win[0][:].indirect(slot_sb[:]), fu[:, 0, :], ALU.mult)
+
+        w1_bf = pool.tile([P, H * PACK], BF16, name="w1_bf", align_bytes=64)
+        w1_codes = pool.tile([P, H], U32, name="w1_codes", align_bytes=64)
+        w1_bytes = pool.tile([P, H], U8, name="w1_bytes", align_bytes=64)
+        w1_dealt = w1_bf[:].rearrange("p (t m r) -> p m r t", t=PACK, r=PACK)
+        nc.vector.tensor_copy(w1_dealt[:, : P // 2], w1_raw[0][:].rearrange("p r (m t) -> p m r t", t=PACK))
+        nc.vector.tensor_copy(x_bytes[:], xs_win[:].indirect(offs_sb[:]))
+        nc.vector.tensor_tensor(spent[:, 0, :], gone_win[0][:].indirect(slot_sb[:]), fd[:, 0, :], ALU.mult)
+        nc.vector.tensor_copy(w1_dealt[:, P // 2 :], w1_raw[1][:].rearrange("p r (m t) -> p m r t", t=PACK))
+        nc.vector.tensor_tensor(used[:, 1, :], use_win[1][:].indirect(slot_sb[:]), fu[:, 1, :], ALU.mult)
+        nc.vector.quantize_mx(out=w1_codes[:].bitcast(FP8X4), scales=w1_bytes[:], in_=w1_bf[:])
+        for t in range(1, PACK):
+            if t > 1:
+                nc.vector.tensor_tensor(used[:, t, :], use_win[t][:].indirect(slot_sb[:]), fu[:, t, :], ALU.mult)
+            nc.vector.tensor_tensor(spent[:, t, :], gone_win[t][:].indirect(slot_sb[:]), fd[:, t, :], ALU.mult)
+
+        act = pool.tile([P, PACK, S], F32, name="act")
+        keep = pool.tile([P, PACK, S], F32, name="keep")
+        rest = pool.tile([P, PACK, S], F32, name="rest")
+        for t in range(PACK):
+            pre = psum.tile([P, S], F32, name="pre%d" % t)
+            cols = slice(t * P, (t + 1) * P)
+            nc.tensor.matmul_mx(
+                out=pre[:],
+                lhsT=w1_codes[:, cols].bitcast(FP8X4),
+                lhsT_scale=w1_bytes[:, cols],
+                rhs=x_codes[:].bitcast(FP8X4),
+                rhs_scale=x_bytes[:],
+                start=True,
+                stop=True,
+            )
+            nc.scalar.activation(act[:, t, :], pre[:], ACT.Sigmoid)
+            nc.scalar.activation(
+                keep[:, t, :], act[:, t, :], ACT.Identity,
+                bias=neg_unit[:, t : t + 1], scale=unit_base[:, t : t + 1],
+            )
+            nc.vector.scalar_tensor_tensor(
+                rest[:, t, :], used[:, t, :], base_m1[:, t : t + 1], keep[:, t, :], ALU.add, ALU.mult
+            )
+
+        w2_bf = pool.tile([P, N * PACK], BF16, name="w2_bf", align_bytes=64)
+        w2_codes = pool.tile([P, N], U32, name="w2_codes", align_bytes=64)
+        w2_bytes = pool.tile([P, N], U8, name="w2_bytes", align_bytes=64)
+        nc.scalar.copy(
+            w2_bf[:].rearrange("p (c i r) -> p c r i", i=4, r=PACK),
+            w2_raw[:].rearrange("p r (c i) -> p c r i", i=4),
+        )
+        nc.vector.quantize_mx(out=w2_codes[:].bitcast(FP8X4), scales=w2_bytes[:], in_=w2_bf[:])
+
+        def release(n):
+            j0, width = CHUNKS[n]
+            cols = slice(j0, j0 + width)
+            avail = pool.tile([P, PACK, width], F32, name="avail%d" % n)
+            z = pool.tile([P, PACK, width], F32, name="z%d" % n)
+            z_bf = pool.tile([P, width * PACK], BF16, name="z_bf%d" % n, align_bytes=64)
+            nc.vector.scalar_tensor_tensor(
+                avail[:], spent[:, :, cols], -1.0, act[:, :, cols], ALU.add, ALU.mult
+            )
+            for t in range(PACK):
+                nc.vector.scalar_tensor_tensor(
+                    z[:, t, :], rest[:, t, cols], neg_unit[:, t : t + 1], avail[:, t, :], ALU.add, ALU.mult
+                )
+            nc.scalar.copy(
+                z_bf[:].rearrange("p (c i r) -> p c r i", i=4, r=PACK),
+                z[:].rearrange("p r (c i) -> p c r i", i=4),
+            )
+            return z_bf
+
+        def product(n, z_bf):
+            width = CHUNKS[n][1]
+            z_codes = pool.tile([P, width], U32, name="z_codes%d" % n, align_bytes=64)
+            z_bytes = pool.tile([P, width], U8, name="z_bytes%d" % n, align_bytes=64)
+            acc = psum.tile([P, width], F32, name="acc%d" % n)
+            nc.vector.quantize_mx(out=z_codes[:].bitcast(FP8X4), scales=z_bytes[:], in_=z_bf[:])
+            nc.tensor.matmul_mx(
+                out=acc[:],
+                lhsT=w2_codes[:].bitcast(FP8X4),
+                lhsT_scale=w2_bytes[:],
+                rhs=z_codes[:].bitcast(FP8X4),
+                rhs_scale=z_bytes[:],
+                start=True,
+                stop=True,
+            )
+            return acc
+
+        def finish(n, acc):
+            j0, width = CHUNKS[n]
+            cols = slice(j0, j0 + width)
+            total = pool.tile([P, width], F32, name="total%d" % n)
+            result = pool.tile([P, width], F32, name="result%d" % n)
+            nc.vector.tensor_tensor(total[:], acc[:], drive_sb[:, cols], ALU.add)
+            nc.scalar.activation(result[:], total[:], ACT.Tanh)
+            nc.sync.dma_start(out=out[:, cols], in_=result[:])
+
+        staged = {}
+        sums = {}
+        for step in range(len(CHUNKS) + 2):
+            if step < len(CHUNKS):
+                staged[step] = release(step)
+            if 1 <= step <= len(CHUNKS):
+                sums[step - 1] = product(step - 1, staged[step - 1])
+            if step >= 2:
+                finish(step - 2, sums[step - 2])

@@ -17,6 +17,7 @@ ACT = mybir.ActivationFunctionType
 
 P = 128
 PACK = 4
+LINE = 4
 CHUNKS = ((0, 256), (256, 128), (384, 128))
 
 
@@ -49,10 +50,11 @@ def tile_picked_ystp_tanh_p_kernel(
                 out=xs_win[32 * q : 32 * q + 4, :].bitcast(I32),
                 in_=x_scales[0, 4 * q : 4 * q + 4, :].bitcast(I32),
             )
-        for queue, col, vec in (
-            (nc.scalar, rf_sb, rf), (nc.scalar, rd_sb, rd), (nc.gpsimd, base_sb, base), (nc.gpsimd, unit_sb, unit)
-        ):
+        def load_rows(queue, col, vec):
             queue.dma_start(out=col[:], in_=vec.rearrange("(p t) o -> p (t o)", t=PACK))
+
+        load_rows(nc.scalar, rf_sb, rf)
+        load_rows(nc.gpsimd, rd_sb, rd)
 
         use_rows = use.rearrange("(p t) u -> p t u", t=PACK)
         gone_rows = gone.rearrange("(p t) u -> p t u", t=PACK)
@@ -67,24 +69,25 @@ def tile_picked_ystp_tanh_p_kernel(
         nc.sync.dma_start(out=w1_raw[0][:], in_=w1_rows[:, :, : H // 2])
         nc.sync.dma_start(out=gone_win[0][:], in_=gone_rows[:, 0, :])
         nc.sync.dma_start(out=w1_raw[1][:], in_=w1_rows[:, :, H // 2 :])
-        for t in range(1, PACK):
+        for t in range(1, PACK - 1):
             nc.sync.dma_start(out=use_win[t][:], in_=use_rows[:, t, :])
+            load_rows(nc.sync, *((base_sb, base), (unit_sb, unit))[t - 1])
             nc.sync.dma_start(out=gone_win[t][:], in_=gone_rows[:, t, :])
+        nc.sync.dma_start(out=gone_win[PACK - 1][:], in_=gone_rows[:, PACK - 1, :])
+        nc.sync.dma_start(out=use_win[PACK - 1][:], in_=use_rows[:, PACK - 1, :])
         nc.sync.dma_start(out=w2_raw[:], in_=w2.rearrange("(p r) c -> p r c", r=PACK))
         nc.sync.dma_start(out=drive_sb[:], in_=drive)
 
-        base_m1 = pool.tile([P, PACK], F32, name="base_m1")
-        unit_base = pool.tile([P, PACK], F32, name="unit_base")
-        neg_unit = pool.tile([P, PACK], F32, name="neg_unit")
-        nc.gpsimd.tensor_scalar(base_m1[:], base_sb[:], 1.0, -1.0, ALU.mult, ALU.add)
-        nc.gpsimd.tensor_tensor(unit_base[:], unit_sb[:], base_sb[:], ALU.mult)
-        nc.gpsimd.tensor_scalar(neg_unit[:], unit_sb[:], -1.0, 0.0, ALU.mult, ALU.add)
-
-        fu = pool.tile([P, PACK, S], F32, name="fu")
-        fd = pool.tile([P, PACK, S], F32, name="fd")
+        fu = [pool.tile([P, S], F32, name="fu%d" % t) for t in range(PACK)]
+        fd = [pool.tile([P, S], F32, name="fd%d" % t) for t in range(PACK)]
         for t in range(PACK):
-            nc.scalar.activation(fu[:, t, :], gap_sb[:], ACT.Exp, scale=rf_sb[:, t : t + 1])
-            nc.scalar.activation(fd[:, t, :], gap_sb[:], ACT.Exp, scale=rd_sb[:, t : t + 1])
+            nc.scalar.activation(fu[t][:], gap_sb[:], ACT.Exp, scale=rf_sb[:, t : t + 1])
+            nc.scalar.activation(fd[t][:], gap_sb[:], ACT.Exp, scale=rd_sb[:, t : t + 1])
+
+        base_m1 = pool.tile([P, PACK], F32, name="base_m1")
+        neg_unit = pool.tile([P, PACK], F32, name="neg_unit")
+        nc.scalar.activation(base_m1[:], base_sb[:], ACT.Identity, bias=-1.0)
+        nc.scalar.activation(neg_unit[:], unit_sb[:], ACT.Copy, scale=-1.0)
 
         x_bytes = pool.tile([P, S], U8, name="x_bytes", align_bytes=64)
         x_codes = pool.tile([P, S], U32, name="x_codes", align_bytes=64)
@@ -92,7 +95,7 @@ def tile_picked_ystp_tanh_p_kernel(
 
         used = pool.tile([P, PACK, S], F32, name="used")
         spent = pool.tile([P, PACK, S], F32, name="spent")
-        nc.vector.tensor_tensor(used[:, 0, :], use_win[0][:].indirect(slot_sb[:]), fu[:, 0, :], ALU.mult)
+        nc.vector.tensor_tensor(used[:, 0, :], use_win[0][:].indirect(slot_sb[:]), fu[0][:], ALU.mult)
 
         w1_bf = pool.tile([P, H * PACK], BF16, name="w1_bf", align_bytes=64)
         w1_codes = pool.tile([P, H], U32, name="w1_codes", align_bytes=64)
@@ -100,18 +103,20 @@ def tile_picked_ystp_tanh_p_kernel(
         w1_dealt = w1_bf[:].rearrange("p (t m r) -> p m r t", t=PACK, r=PACK)
         nc.vector.tensor_copy(w1_dealt[:, : P // 2], w1_raw[0][:].rearrange("p r (m t) -> p m r t", t=PACK))
         nc.vector.tensor_copy(x_bytes[:], xs_win[:].indirect(offs_sb[:]))
-        nc.vector.tensor_tensor(spent[:, 0, :], gone_win[0][:].indirect(slot_sb[:]), fd[:, 0, :], ALU.mult)
+        nc.vector.tensor_tensor(spent[:, 0, :], gone_win[0][:].indirect(slot_sb[:]), fd[0][:], ALU.mult)
         nc.vector.tensor_copy(w1_dealt[:, P // 2 :], w1_raw[1][:].rearrange("p r (m t) -> p m r t", t=PACK))
-        nc.vector.tensor_tensor(used[:, 1, :], use_win[1][:].indirect(slot_sb[:]), fu[:, 1, :], ALU.mult)
         nc.vector.quantize_mx(out=w1_codes[:].bitcast(FP8X4), scales=w1_bytes[:], in_=w1_bf[:])
-        for t in range(1, PACK):
-            if t > 1:
-                nc.vector.tensor_tensor(used[:, t, :], use_win[t][:].indirect(slot_sb[:]), fu[:, t, :], ALU.mult)
-            nc.vector.tensor_tensor(spent[:, t, :], gone_win[t][:].indirect(slot_sb[:]), fd[:, t, :], ALU.mult)
+        nc.vector.tensor_tensor(used[:, 1, :], use_win[1][:].indirect(slot_sb[:]), fu[1][:], ALU.mult)
+        nc.vector.tensor_tensor(spent[:, 1, :], gone_win[1][:].indirect(slot_sb[:]), fd[1][:], ALU.mult)
+        nc.vector.tensor_tensor(used[:, 2, :], use_win[2][:].indirect(slot_sb[:]), fu[2][:], ALU.mult)
+        nc.vector.tensor_tensor(spent[:, 2, :], gone_win[2][:].indirect(slot_sb[:]), fd[2][:], ALU.mult)
+        nc.vector.tensor_tensor(spent[:, 3, :], gone_win[3][:].indirect(slot_sb[:]), fd[3][:], ALU.mult)
+        nc.vector.tensor_tensor(used[:, 3, :], use_win[3][:].indirect(slot_sb[:]), fu[3][:], ALU.mult)
 
         act = pool.tile([P, PACK, S], F32, name="act")
         keep = pool.tile([P, PACK, S], F32, name="keep")
-        rest = pool.tile([P, PACK, S], F32, name="rest")
+        fired = pool.tile([P, S // LINE, PACK, LINE], F32, name="fired")
+        store = pool.tile([P, S // LINE, PACK, LINE], F32, name="store")
         for t in range(PACK):
             pre = psum.tile([P, S], F32, name="pre%d" % t)
             cols = slice(t * P, (t + 1) * P)
@@ -126,11 +131,27 @@ def tile_picked_ystp_tanh_p_kernel(
             )
             nc.scalar.activation(act[:, t, :], pre[:], ACT.Sigmoid)
             nc.scalar.activation(
-                keep[:, t, :], act[:, t, :], ACT.Identity,
-                bias=neg_unit[:, t : t + 1], scale=unit_base[:, t : t + 1],
+                keep[:, t, :], act[:, t, :], ACT.Identity, bias=-1.0, scale=base_sb[:, t : t + 1]
+            )
+            rest = pool.tile([P, S], F32, name="rest%d" % t, tag=("fd2", "fd3", "fu3", "fu2")[t])
+            nc.vector.scalar_tensor_tensor(
+                rest[:], used[:, t, :], base_m1[:, t : t + 1], keep[:, t, :], ALU.add, ALU.mult
             )
             nc.vector.scalar_tensor_tensor(
-                rest[:, t, :], used[:, t, :], base_m1[:, t : t + 1], keep[:, t, :], ALU.add, ALU.mult
+                fired[:, :, t, :],
+                rest[:].rearrange("p (c i) -> p c i", i=LINE),
+                -1.0,
+                act[:, t, :].rearrange("p (c i) -> p c i", i=LINE),
+                ALU.add,
+                ALU.mult,
+            )
+        for t in range(PACK):
+            nc.scalar.activation(
+                store[:, :, t, :],
+                spent[:, t, :].rearrange("p (c i) -> p c i", i=LINE),
+                ACT.Identity,
+                bias=neg_unit[:, t : t + 1],
+                scale=unit_sb[:, t : t + 1],
             )
 
         w2_bf = pool.tile([P, N * PACK], BF16, name="w2_bf", align_bytes=64)
@@ -144,20 +165,13 @@ def tile_picked_ystp_tanh_p_kernel(
 
         def release(n):
             j0, width = CHUNKS[n]
-            cols = slice(j0, j0 + width)
-            avail = pool.tile([P, PACK, width], F32, name="avail%d" % n)
-            z = pool.tile([P, PACK, width], F32, name="z%d" % n)
+            groups = slice(j0 // LINE, (j0 + width) // LINE)
             z_bf = pool.tile([P, width * PACK], BF16, name="z_bf%d" % n, align_bytes=64)
-            nc.vector.scalar_tensor_tensor(
-                avail[:], spent[:, :, cols], -1.0, act[:, :, cols], ALU.add, ALU.mult
-            )
-            for t in range(PACK):
-                nc.vector.scalar_tensor_tensor(
-                    z[:, t, :], rest[:, t, cols], neg_unit[:, t : t + 1], avail[:, t, :], ALU.add, ALU.mult
-                )
-            nc.scalar.copy(
-                z_bf[:].rearrange("p (c i r) -> p c r i", i=4, r=PACK),
-                z[:].rearrange("p r (c i) -> p c r i", i=4),
+            nc.vector.tensor_tensor(
+                z_bf[:].rearrange("p (c i r) -> p c r i", i=LINE, r=PACK),
+                fired[:, groups],
+                store[:, groups],
+                ALU.mult,
             )
             return z_bf
 

@@ -17,7 +17,8 @@ ACT = mybir.ActivationFunctionType
 
 P = 128
 PACK = 4
-LINE = 4
+PAIR = 2
+SCALAR_DEALS = 48
 CHUNKS = ((0, 256), (256, 128), (384, 128))
 
 
@@ -34,7 +35,7 @@ def tile_picked_ystp_tanh_p_kernel(
         xs_win = pool.tile([P, T], U8, name="xs_win")
         xw_win = pool.tile([P, T], U32, name="xw_win")
         gap_sb = pool.tile([P, S], F32, name="gap_sb")
-        w1_raw = [pool.tile([P, PACK, H // 2], F32, name="w1_raw%d" % h) for h in range(2)]
+        w1_raw = pool.tile([P, PACK, H], F32, name="w1_raw")
         w2_raw = pool.tile([P, PACK, N], F32, name="w2_raw")
         drive_sb = pool.tile([P, S], F32, name="drive_sb")
         use_win = [pool.tile([P, U], F32, name="use_win%d" % t) for t in range(PACK)]
@@ -66,23 +67,31 @@ def tile_picked_ystp_tanh_p_kernel(
         )
         nc.sync.dma_start(slot_sb[:], slot)
         nc.sync.dma_start(out=use_win[0][:], in_=use_rows[:, 0, :])
-        nc.sync.dma_start(out=w1_raw[0][:], in_=w1_rows[:, :, : H // 2])
         nc.sync.dma_start(out=gone_win[0][:], in_=gone_rows[:, 0, :])
-        nc.sync.dma_start(out=w1_raw[1][:], in_=w1_rows[:, :, H // 2 :])
-        for t in range(1, PACK - 1):
-            nc.sync.dma_start(out=use_win[t][:], in_=use_rows[:, t, :])
-            load_rows(nc.sync, *((base_sb, base), (unit_sb, unit))[t - 1])
-            nc.sync.dma_start(out=gone_win[t][:], in_=gone_rows[:, t, :])
+        nc.sync.dma_start(out=use_win[1][:], in_=use_rows[:, 1, :])
+        nc.sync.dma_start(out=w1_raw[:], in_=w1_rows)
+        nc.sync.dma_start(out=gone_win[1][:], in_=gone_rows[:, 1, :])
+        load_rows(nc.sync, unit_sb, unit)
+        nc.sync.dma_start(out=use_win[2][:], in_=use_rows[:, 2, :])
+        load_rows(nc.sync, base_sb, base)
+        nc.sync.dma_start(out=gone_win[2][:], in_=gone_rows[:, 2, :])
         nc.sync.dma_start(out=gone_win[PACK - 1][:], in_=gone_rows[:, PACK - 1, :])
         nc.sync.dma_start(out=use_win[PACK - 1][:], in_=use_rows[:, PACK - 1, :])
         nc.sync.dma_start(out=w2_raw[:], in_=w2.rearrange("(p r) c -> p r c", r=PACK))
         nc.sync.dma_start(out=drive_sb[:], in_=drive)
 
+        w1_bf = pool.tile([P, H * PACK], BF16, name="w1_bf", align_bytes=64)
+        w1_codes = pool.tile([P, H], U32, name="w1_codes", align_bytes=64)
+        w1_bytes = pool.tile([P, H], U8, name="w1_bytes", align_bytes=64)
+        w1_dealt = w1_bf[:].rearrange("p (h e m r) -> p h m r e", h=2, e=PAIR, r=PACK)
+        w1_src = w1_raw[:].rearrange("p r (m h e) -> p h m r e", h=2, e=PAIR)
         fu = [pool.tile([P, S], F32, name="fu%d" % t) for t in range(PACK)]
         fd = [pool.tile([P, S], F32, name="fd%d" % t) for t in range(PACK)]
         for t in range(PACK):
             nc.scalar.activation(fu[t][:], gap_sb[:], ACT.Exp, scale=rf_sb[:, t : t + 1])
             nc.scalar.activation(fd[t][:], gap_sb[:], ACT.Exp, scale=rd_sb[:, t : t + 1])
+            if t == 1:
+                nc.scalar.copy(w1_dealt[:, :, :SCALAR_DEALS], w1_src[:, :, :SCALAR_DEALS])
 
         base_m1 = pool.tile([P, PACK], F32, name="base_m1")
         neg_unit = pool.tile([P, PACK], F32, name="neg_unit")
@@ -97,17 +106,12 @@ def tile_picked_ystp_tanh_p_kernel(
         spent = pool.tile([P, PACK, S], F32, name="spent")
         nc.vector.tensor_tensor(used[:, 0, :], use_win[0][:].indirect(slot_sb[:]), fu[0][:], ALU.mult)
 
-        w1_bf = pool.tile([P, H * PACK], BF16, name="w1_bf", align_bytes=64)
-        w1_codes = pool.tile([P, H], U32, name="w1_codes", align_bytes=64)
-        w1_bytes = pool.tile([P, H], U8, name="w1_bytes", align_bytes=64)
-        w1_dealt = w1_bf[:].rearrange("p (t m r) -> p m r t", t=PACK, r=PACK)
-        nc.vector.tensor_copy(w1_dealt[:, : P // 2], w1_raw[0][:].rearrange("p r (m t) -> p m r t", t=PACK))
-        nc.vector.tensor_copy(x_bytes[:], xs_win[:].indirect(offs_sb[:]))
         nc.vector.tensor_tensor(spent[:, 0, :], gone_win[0][:].indirect(slot_sb[:]), fd[0][:], ALU.mult)
-        nc.vector.tensor_copy(w1_dealt[:, P // 2 :], w1_raw[1][:].rearrange("p r (m t) -> p m r t", t=PACK))
-        nc.vector.quantize_mx(out=w1_codes[:].bitcast(FP8X4), scales=w1_bytes[:], in_=w1_bf[:])
         nc.vector.tensor_tensor(used[:, 1, :], use_win[1][:].indirect(slot_sb[:]), fu[1][:], ALU.mult)
+        nc.vector.tensor_copy(x_bytes[:], xs_win[:].indirect(offs_sb[:]))
+        nc.vector.tensor_copy(w1_dealt[:, :, SCALAR_DEALS:], w1_src[:, :, SCALAR_DEALS:])
         nc.vector.tensor_tensor(spent[:, 1, :], gone_win[1][:].indirect(slot_sb[:]), fd[1][:], ALU.mult)
+        nc.vector.quantize_mx(out=w1_codes[:].bitcast(FP8X4), scales=w1_bytes[:], in_=w1_bf[:])
         nc.vector.tensor_tensor(used[:, 2, :], use_win[2][:].indirect(slot_sb[:]), fu[2][:], ALU.mult)
         nc.vector.tensor_tensor(spent[:, 2, :], gone_win[2][:].indirect(slot_sb[:]), fd[2][:], ALU.mult)
         nc.vector.tensor_tensor(spent[:, 3, :], gone_win[3][:].indirect(slot_sb[:]), fd[3][:], ALU.mult)
@@ -115,8 +119,8 @@ def tile_picked_ystp_tanh_p_kernel(
 
         act = pool.tile([P, PACK, S], F32, name="act")
         keep = pool.tile([P, PACK, S], F32, name="keep")
-        fired = pool.tile([P, S // LINE, PACK, LINE], F32, name="fired")
-        store = pool.tile([P, S // LINE, PACK, LINE], F32, name="store")
+        rest = pool.tile([P, PACK, S], F32, name="rest", tag="gone_win3")
+        store = pool.tile([P, PACK, S], F32, name="store")
         for t in range(PACK):
             pre = psum.tile([P, S], F32, name="pre%d" % t)
             cols = slice(t * P, (t + 1) * P)
@@ -133,44 +137,37 @@ def tile_picked_ystp_tanh_p_kernel(
             nc.scalar.activation(
                 keep[:, t, :], act[:, t, :], ACT.Identity, bias=-1.0, scale=base_sb[:, t : t + 1]
             )
-            rest = pool.tile([P, S], F32, name="rest%d" % t, tag=("fd2", "fd3", "fu3", "fu2")[t])
             nc.vector.scalar_tensor_tensor(
-                rest[:], used[:, t, :], base_m1[:, t : t + 1], keep[:, t, :], ALU.add, ALU.mult
-            )
-            nc.vector.scalar_tensor_tensor(
-                fired[:, :, t, :],
-                rest[:].rearrange("p (c i) -> p c i", i=LINE),
-                -1.0,
-                act[:, t, :].rearrange("p (c i) -> p c i", i=LINE),
-                ALU.add,
-                ALU.mult,
+                rest[:, t, :], used[:, t, :], base_m1[:, t : t + 1], keep[:, t, :], ALU.add, ALU.mult
             )
         for t in range(PACK):
             nc.scalar.activation(
-                store[:, :, t, :],
-                spent[:, t, :].rearrange("p (c i) -> p c i", i=LINE),
-                ACT.Identity,
-                bias=neg_unit[:, t : t + 1],
-                scale=unit_sb[:, t : t + 1],
+                store[:, t, :], spent[:, t, :], ACT.Identity, bias=neg_unit[:, t : t + 1], scale=unit_sb[:, t : t + 1]
             )
 
         w2_bf = pool.tile([P, N * PACK], BF16, name="w2_bf", align_bytes=64)
         w2_codes = pool.tile([P, N], U32, name="w2_codes", align_bytes=64)
         w2_bytes = pool.tile([P, N], U8, name="w2_bytes", align_bytes=64)
         nc.scalar.copy(
-            w2_bf[:].rearrange("p (c i r) -> p c r i", i=4, r=PACK),
-            w2_raw[:].rearrange("p r (c i) -> p c r i", i=4),
+            w2_bf[:].rearrange("p (c i r) -> p c r i", i=PAIR, r=PACK),
+            w2_raw[:].rearrange("p r (c i) -> p c r i", i=PAIR),
         )
         nc.vector.quantize_mx(out=w2_codes[:].bitcast(FP8X4), scales=w2_bytes[:], in_=w2_bf[:])
 
-        def release(n):
+        def fire(n):
             j0, width = CHUNKS[n]
-            groups = slice(j0 // LINE, (j0 + width) // LINE)
+            cols = slice(j0, j0 + width)
+            fired = pool.tile([P, PACK, width], F32, name="fired%d" % n)
+            nc.vector.scalar_tensor_tensor(fired[:], rest[:, :, cols], -1.0, act[:, :, cols], ALU.add, ALU.mult)
+            return fired
+
+        def release(n, fired):
+            j0, width = CHUNKS[n]
             z_bf = pool.tile([P, width * PACK], BF16, name="z_bf%d" % n, align_bytes=64)
             nc.vector.tensor_tensor(
-                z_bf[:].rearrange("p (c i r) -> p c r i", i=LINE, r=PACK),
-                fired[:, groups],
-                store[:, groups],
+                z_bf[:].rearrange("p (c i r) -> p c r i", i=PAIR, r=PACK),
+                fired[:].rearrange("p r (c i) -> p c r i", i=PAIR),
+                store[:, :, j0 : j0 + width].rearrange("p r (c i) -> p c r i", i=PAIR),
                 ALU.mult,
             )
             return z_bf
@@ -201,12 +198,10 @@ def tile_picked_ystp_tanh_p_kernel(
             nc.scalar.activation(result[:], total[:], ACT.Tanh)
             nc.sync.dma_start(out=out[:, cols], in_=result[:])
 
-        staged = {}
-        sums = {}
-        for step in range(len(CHUNKS) + 2):
-            if step < len(CHUNKS):
-                staged[step] = release(step)
-            if 1 <= step <= len(CHUNKS):
-                sums[step - 1] = product(step - 1, staged[step - 1])
-            if step >= 2:
-                finish(step - 2, sums[step - 2])
+        stages = (fire, release, product, finish)
+        carried = {}
+        for step in range(len(CHUNKS) + len(stages) - 1):
+            for depth, stage in enumerate(stages):
+                n = step - depth
+                if 0 <= n < len(CHUNKS):
+                    carried[n] = stage(n, carried[n]) if depth else stage(n)

from contextlib import ExitStack

import concourse.mybir as mybir

K, T, S, H, N, U = 512, 1024, 512, 512, 128, 1024
FLOPS = 2 * K * H * S + 2 * H * N * S

F32 = mybir.dt.float32
BF16 = mybir.dt.bfloat16
I32 = mybir.dt.int32
U32 = mybir.dt.uint32
U16 = mybir.dt.uint16
U8 = mybir.dt.uint8
FP8X4 = mybir.dt.float8_e4m3fn_x4
ALU = mybir.AluOpType
ACT = mybir.ActivationFunctionType

P = 128
PACK = 4
PAIR = 2
SCALAR_DEALS = 48
CHUNKS = ((0, 256), (256, 128), (384, 128))


def tile_picked_ystp_tanh_p_kernel(
    tc, x_words, x_scales, w1, gap, base, rf, rd, use, gone, w2, unit, drive, offs, slot, out
):
    nc = tc.nc
    with ExitStack() as ctx:
        pool = ctx.enter_context(tc.tile_pool(name="keep", bufs=1))
        psum = ctx.enter_context(tc.psum_pool(name="psum", bufs=1))

        offs_sb = pool.tile([P, S // 16], U16, name="offs_sb")
        slot_sb = pool.tile([P, S // 16], U16, name="slot_sb")
        xs_win = pool.tile([P, T], U8, name="xs_win")
        xw_win = pool.tile([P, T], U32, name="xw_win")
        gap_sb = pool.tile([P, S], F32, name="gap_sb")
        w1_raw = pool.tile([P, PACK, H], F32, name="w1_raw")
        w2_raw = pool.tile([P, PACK, N], F32, name="w2_raw")
        drive_sb = pool.tile([P, S], F32, name="drive_sb")
        use_win = [pool.tile([P, U], F32, name="use_win%d" % t) for t in range(PACK)]
        gone_win = [pool.tile([P, U], F32, name="gone_win%d" % t) for t in range(PACK)]
        rf_sb = pool.tile([P, PACK], F32, name="rf_sb")
        rd_sb = pool.tile([P, PACK], F32, name="rd_sb")
        base_sb = pool.tile([P, PACK], F32, name="base_sb")
        unit_sb = pool.tile([P, PACK], F32, name="unit_sb")

        nc.gpsimd.memset(xs_win[:].bitcast(I32), 0)
        for q in range(4):
            nc.scalar.dma_start(
                out=xs_win[32 * q : 32 * q + 4, :].bitcast(I32),
                in_=x_scales[0, 4 * q : 4 * q + 4, :].bitcast(I32),
            )
        def load_rows(queue, col, vec):
            queue.dma_start(out=col[:], in_=vec.rearrange("(p t) o -> p (t o)", t=PACK))

        load_rows(nc.scalar, rf_sb, rf)
        load_rows(nc.gpsimd, rd_sb, rd)

        use_rows = use.rearrange("(p t) u -> p t u", t=PACK)
        gone_rows = gone.rearrange("(p t) u -> p t u", t=PACK)
        w1_rows = w1.rearrange("(p r) c -> p r c", r=PACK)
        nc.sync.dma_start(offs_sb[:], offs)
        nc.sync.dma_start(out=gap_sb[:], in_=gap)
        nc.sync.dma_start(
            out=xw_win[:].bitcast(I32), in_=x_words[0].rearrange("p n r -> p (n r)").bitcast(I32)
        )
        nc.sync.dma_start(slot_sb[:], slot)
        nc.sync.dma_start(out=use_win[0][:], in_=use_rows[:, 0, :])
        nc.sync.dma_start(out=gone_win[0][:], in_=gone_rows[:, 0, :])
        nc.sync.dma_start(out=use_win[1][:], in_=use_rows[:, 1, :])
        nc.sync.dma_start(out=w1_raw[:], in_=w1_rows)
        nc.sync.dma_start(out=gone_win[1][:], in_=gone_rows[:, 1, :])
        load_rows(nc.sync, unit_sb, unit)
        nc.sync.dma_start(out=use_win[2][:], in_=use_rows[:, 2, :])
        load_rows(nc.sync, base_sb, base)
        nc.sync.dma_start(out=gone_win[2][:], in_=gone_rows[:, 2, :])
        nc.sync.dma_start(out=gone_win[PACK - 1][:], in_=gone_rows[:, PACK - 1, :])
        nc.sync.dma_start(out=use_win[PACK - 1][:], in_=use_rows[:, PACK - 1, :])
        nc.sync.dma_start(out=w2_raw[:], in_=w2.rearrange("(p r) c -> p r c", r=PACK))
        nc.sync.dma_start(out=drive_sb[:], in_=drive)

        w1_bf = pool.tile([P, H * PACK], BF16, name="w1_bf", align_bytes=64)
        w1_codes = pool.tile([P, H], U32, name="w1_codes", align_bytes=64)
        w1_bytes = pool.tile([P, H], U8, name="w1_bytes", align_bytes=64)
        w1_dealt = w1_bf[:].rearrange("p (h e m r) -> p h m r e", h=2, e=PAIR, r=PACK)
        w1_src = w1_raw[:].rearrange("p r (m h e) -> p h m r e", h=2, e=PAIR)
        fu = [pool.tile([P, S], F32, name="fu%d" % t) for t in range(PACK)]
        fd = [pool.tile([P, S], F32, name="fd%d" % t) for t in range(PACK)]
        for t in range(PACK):
            nc.scalar.activation(fu[t][:], gap_sb[:], ACT.Exp, scale=rf_sb[:, t : t + 1])
            nc.scalar.activation(fd[t][:], gap_sb[:], ACT.Exp, scale=rd_sb[:, t : t + 1])
            if t == 1:
                nc.scalar.copy(w1_dealt[:, :, :SCALAR_DEALS], w1_src[:, :, :SCALAR_DEALS])

        base_m1 = pool.tile([P, PACK], F32, name="base_m1")
        neg_unit = pool.tile([P, PACK], F32, name="neg_unit")
        nc.scalar.activation(base_m1[:], base_sb[:], ACT.Identity, bias=-1.0)
        nc.scalar.activation(neg_unit[:], unit_sb[:], ACT.Copy, scale=-1.0)

        x_bytes = pool.tile([P, S], U8, name="x_bytes", align_bytes=64)
        x_codes = pool.tile([P, S], U32, name="x_codes", align_bytes=64)
        nc.vector.tensor_copy(x_codes[:], xw_win[:].indirect(offs_sb[:]))

        used = pool.tile([P, PACK, S], F32, name="used")
        spent = pool.tile([P, PACK, S], F32, name="spent")
        nc.vector.tensor_tensor(used[:, 0, :], use_win[0][:].indirect(slot_sb[:]), fu[0][:], ALU.mult)

        nc.vector.tensor_tensor(spent[:, 0, :], gone_win[0][:].indirect(slot_sb[:]), fd[0][:], ALU.mult)
        nc.vector.tensor_tensor(used[:, 1, :], use_win[1][:].indirect(slot_sb[:]), fu[1][:], ALU.mult)
        nc.vector.tensor_copy(x_bytes[:], xs_win[:].indirect(offs_sb[:]))
        nc.vector.tensor_copy(w1_dealt[:, :, SCALAR_DEALS:], w1_src[:, :, SCALAR_DEALS:])
        nc.vector.tensor_tensor(spent[:, 1, :], gone_win[1][:].indirect(slot_sb[:]), fd[1][:], ALU.mult)
        nc.vector.quantize_mx(out=w1_codes[:].bitcast(FP8X4), scales=w1_bytes[:], in_=w1_bf[:])
        nc.vector.tensor_tensor(used[:, 2, :], use_win[2][:].indirect(slot_sb[:]), fu[2][:], ALU.mult)
        nc.vector.tensor_tensor(spent[:, 2, :], gone_win[2][:].indirect(slot_sb[:]), fd[2][:], ALU.mult)
        nc.vector.tensor_tensor(spent[:, 3, :], gone_win[3][:].indirect(slot_sb[:]), fd[3][:], ALU.mult)
        nc.vector.tensor_tensor(used[:, 3, :], use_win[3][:].indirect(slot_sb[:]), fu[3][:], ALU.mult)

        act = pool.tile([P, PACK, S], F32, name="act")
        keep = pool.tile([P, PACK, S], F32, name="keep")
        rest = pool.tile([P, PACK, S], F32, name="rest", tag="gone_win3")
        store = pool.tile([P, PACK, S], F32, name="store")
        for t in range(PACK):
            pre = psum.tile([P, S], F32, name="pre%d" % t)
            cols = slice(t * P, (t + 1) * P)
            nc.tensor.matmul_mx(
                out=pre[:],
                lhsT=w1_codes[:, cols].bitcast(FP8X4),
                lhsT_scale=w1_bytes[:, cols],
                rhs=x_codes[:].bitcast(FP8X4),
                rhs_scale=x_bytes[:],
                start=True,
                stop=True,
            )
            nc.scalar.activation(act[:, t, :], pre[:], ACT.Sigmoid)
            nc.scalar.activation(
                keep[:, t, :], act[:, t, :], ACT.Identity, bias=-1.0, scale=base_sb[:, t : t + 1]
            )
            nc.vector.scalar_tensor_tensor(
                rest[:, t, :], used[:, t, :], base_m1[:, t : t + 1], keep[:, t, :], ALU.add, ALU.mult
            )
        for t in range(PACK):
            nc.scalar.activation(
                store[:, t, :], spent[:, t, :], ACT.Identity, bias=neg_unit[:, t : t + 1], scale=unit_sb[:, t : t + 1]
            )

        w2_bf = pool.tile([P, N * PACK], BF16, name="w2_bf", align_bytes=64)
        w2_codes = pool.tile([P, N], U32, name="w2_codes", align_bytes=64)
        w2_bytes = pool.tile([P, N], U8, name="w2_bytes", align_bytes=64)
        nc.scalar.copy(
            w2_bf[:].rearrange("p (c i r) -> p c r i", i=PAIR, r=PACK),
            w2_raw[:].rearrange("p r (c i) -> p c r i", i=PAIR),
        )
        nc.vector.quantize_mx(out=w2_codes[:].bitcast(FP8X4), scales=w2_bytes[:], in_=w2_bf[:])

        def fire(n):
            j0, width = CHUNKS[n]
            cols = slice(j0, j0 + width)
            fired = pool.tile([P, PACK, width], F32, name="fired%d" % n)
            nc.vector.scalar_tensor_tensor(fired[:], rest[:, :, cols], -1.0, act[:, :, cols], ALU.add, ALU.mult)
            return fired

        def release(n, fired):
            j0, width = CHUNKS[n]
            z_bf = pool.tile([P, width * PACK], BF16, name="z_bf%d" % n, align_bytes=64)
            nc.vector.tensor_tensor(
                z_bf[:].rearrange("p (c i r) -> p c r i", i=PAIR, r=PACK),
                fired[:].rearrange("p r (c i) -> p c r i", i=PAIR),
                store[:, :, j0 : j0 + width].rearrange("p r (c i) -> p c r i", i=PAIR),
                ALU.mult,
            )
            return z_bf

        def product(n, z_bf):
            width = CHUNKS[n][1]
            z_codes = pool.tile([P, width], U32, name="z_codes%d" % n, align_bytes=64)
            z_bytes = pool.tile([P, width], U8, name="z_bytes%d" % n, align_bytes=64)
            acc = psum.tile([P, width], F32, name="acc%d" % n)
            nc.vector.quantize_mx(out=z_codes[:].bitcast(FP8X4), scales=z_bytes[:], in_=z_bf[:])
            nc.tensor.matmul_mx(
                out=acc[:],
                lhsT=w2_codes[:].bitcast(FP8X4),
                lhsT_scale=w2_bytes[:],
                rhs=z_codes[:].bitcast(FP8X4),
                rhs_scale=z_bytes[:],
                start=True,
                stop=True,
            )
            return acc

        def finish(n, acc):
            j0, width = CHUNKS[n]
            cols = slice(j0, j0 + width)
            total = pool.tile([P, width], F32, name="total%d" % n)
            result = pool.tile([P, width], F32, name="result%d" % n)
            nc.vector.tensor_tensor(total[:], acc[:], drive_sb[:, cols], ALU.add)
            nc.scalar.activation(result[:], total[:], ACT.Tanh)
            nc.sync.dma_start(out=out[:, cols], in_=result[:])

        stages = (fire, release, product, finish)
        carried = {}
        for step in range(len(CHUNKS) + len(stages) - 1):
            for depth, stage in enumerate(stages):
                n = step - depth
                if 0 <= n < len(CHUNKS):
                    carried[n] = stage(n, carried[n]) if depth else stage(n)
